import numpy as np
import ml_dtypes


def mxq(x, axis, fmt="e4m3"):
    dtype, down = {"e4m3": (ml_dtypes.float8_e4m3fn, 7), "e5m2": (ml_dtypes.float8_e5m2, 14)}[fmt]
    v = np.moveaxis(np.asarray(x, np.float32).astype(ml_dtypes.bfloat16).astype(np.float64), axis, -1)
    blocks = v.reshape(v.shape[:-1] + (-1, 32))
    amax = np.abs(blocks).max(-1, keepdims=True)
    byte = np.maximum(np.where(amax > 0, np.frexp(amax)[1] - 1 + 127, 0) - down, 1)
    scale = np.exp2(byte - 127.0)
    codes = (blocks / scale).astype(np.float32).astype(dtype).astype(np.float64)
    return np.moveaxis((codes * scale).reshape(v.shape), -1, axis)


WIDE = False


def mx_kscale(k):
    if not WIDE:
        return np.ones(k)
    levels = np.array([10, -10, 5, -5, 0])
    if k % 512:
        return np.exp2(np.random.permutation(np.resize(levels, k // 32))).repeat(32)
    a = np.empty((k // 512, 16))
    for p in range(k // 512):
        a[p, :8] = np.random.permutation(np.resize(levels, 8))
        for g in range(8):
            far = levels[np.abs(levels - a[p, g]) >= 10]
            a[p, g + 8] = far[np.random.randint(len(far))]
    return np.exp2(a.ravel()).repeat(32)


def f64(x):
    return np.asarray(x).astype(np.float64)


def striped(idx):
    return np.tile(np.asarray(idx).reshape(-1, 16).T, (8, 1)).astype(np.uint16)


def unstriped(offs):
    return offs[:16].T.reshape(-1).astype(np.int64)


E2M1 = np.array([0.0, 0.5, 1.0, 1.5, 2.0, 3.0, 4.0, 6.0, -0.0, -0.5, -1.0, -1.5, -2.0, -3.0, -4.0, -6.0])


def pack_weight(w, fmt):
    k, n = w.shape
    w = f64(np.asarray(w, np.float32).astype(ml_dtypes.bfloat16)).reshape(k // 32, 32, n)
    amax = np.abs(w).max(1)
    if fmt == "e4m3":
        byte = np.frexp(amax)[1] - 1 + 127 - 7
    else:
        mant, ex = np.frexp(amax / 6.0)
        byte = np.where(mant > 0.5, ex, ex - 1) + 127
    byte = np.clip(np.where(amax > 0, byte, 1), 1, 254)
    scaled = (w * np.exp2(127.0 - byte)[:, None, :]).reshape(k, n).astype(np.float32)
    by_word = np.ascontiguousarray(scaled.reshape(k // 512, 128, 4, n).transpose(0, 1, 3, 2))
    if fmt == "e4m3":
        words = by_word.astype(ml_dtypes.float8_e4m3fn).view(np.uint8)
    else:
        c = by_word.astype(ml_dtypes.float4_e2m1fn).view(np.uint8) & 0xF
        words = (c[..., 0::2] | (c[..., 1::2] << 4)).reshape(k // 512, 128, 2 * n)
    return np.ascontiguousarray(words), np.ascontiguousarray(byte.astype(np.uint8).reshape(k // 512, 16, n))


def unpack_weight(words, scales, fmt):
    g, _, n = scales.shape
    words = np.ascontiguousarray(words).reshape(g, 128, n, -1)
    if fmt == "e4m3":
        vals = words.view(ml_dtypes.float8_e4m3fn).astype(np.float64)
    else:
        nib = np.empty((g, 128, n, 4), np.uint8)
        nib[..., 0::2] = words & 0xF
        nib[..., 1::2] = words >> 4
        vals = E2M1[nib]
    vals = vals * np.repeat(np.exp2(scales.astype(np.float64) - 127.0), 8, axis=1)[..., None]
    return vals.transpose(0, 1, 3, 2).reshape(g * 512, n)


def softplus(v):
    return np.log(1.0 + np.exp(v))


B, N, T, D, NQ = 1, 512, 2048, 512, 256


def setup_inputs():
    n = np.random.standard_normal
    idx = np.random.permutation(T)[:B * N]
    s = mx_kscale(D)[:, None]
    kp = pack_weight(n((D, T)) / s, "e4m3")
    return {
        "qT": (n((B, D, NQ)) * s * (1.00 / np.sqrt(D))).astype(np.float32),
        "k_words": kp[0],
        "k_scales": kp[1],
        "ib": np.tile(0.5 * n(2048), (128, 1)).astype(np.float32),
        "ps": (n((B, NQ, 1)) + 1).astype(np.float32),
        "offs": striped(idx),
    }


def reference(qT, k_words, k_scales, ib, ps, offs):
    idx = unstriped(offs)
    pick = lambda x, which: x[:, which].reshape(x.shape[0], B, -1).transpose(1, 0, 2)
    k = unpack_weight(k_words, k_scales, "e4m3")
    kg = pick(k, idx)
    qq = mxq(f64(qT), 1, "e4m3")
    a = qq.transpose(0, 2, 1) @ kg
    y = softplus(a + pick(f64(ib), idx)[:, :1, :] - f64(ps))
    return y

@@ -1,0 +1,120 @@
+from contextlib import ExitStack
+
+import concourse.mybir as mybir
+from concourse.masks import make_identity
+
+T, D, NQ, N = 2048, 512, 256, 512
+FLOPS = 2 * NQ * N * D
+
+F32 = mybir.dt.float32
+BF16 = mybir.dt.bfloat16
+I32 = mybir.dt.int32
+U32 = mybir.dt.uint32
+U16 = mybir.dt.uint16
+U8 = mybir.dt.uint8
+FP8X4 = mybir.dt.float8_e4m3fn_x4
+ACT = mybir.ActivationFunctionType
+ALU = mybir.AluOpType
+
+P = 128
+PACK = 4
+QB = NQ // P
+HALF = N // 2
+BIAS_ROW = P - 1
+EXP_CAP = 2.0**60
+
+
+def tile_attend_bpr_topk_kernel(tc, qT, k_words, k_scales, ib, ps, offs, out):
+    nc = tc.nc
+    with ExitStack() as ctx:
+        sb = ctx.enter_context(tc.tile_pool(name="sb", bufs=1))
+        psum = ctx.enter_context(tc.psum_pool(name="psum", bufs=1))
+
+        offsets = sb.tile([P, N // 16], U16, name="offsets")
+        bias_pool = sb.tile([P, T], F32, name="bias_pool")
+        scale_pool = sb.tile([P, T // 4], I32, name="scale_pool")
+        word_pool = sb.tile([P, T], I32, name="word_pool")
+        q_raw = sb.tile([P, PACK, NQ], F32, name="q_raw")
+        pos = sb.tile([P, QB], F32, name="pos")
+        zero = sb.tile([P, 1], F32, name="zero")
+        ident = sb.tile([P, P], F32, name="ident")
+        v = sb.tile([P, QB * N + 1], F32, name="v")
+        e = sb.tile([P, QB * N + 1], F32, name="e")
+        lg = sb.tile([P, QB * N], F32, name="lg")
+        res = sb.tile([P, QB * N], F32, name="res")
+
+        nc.vector.memset(scale_pool[:], 0)
+        nc.vector.memset(bias_pool[0:BIAS_ROW, :], 0.0)
+        nc.gpsimd.memset(zero[:], 0.0)
+        nc.scalar.activation(v[:, QB * N : QB * N + 1], zero[:], ACT.Copy)
+        make_identity(nc, ident[:])
+
+        nc.sync.dma_start(offsets[:], offs)
+        nc.sync.dma_start(bias_pool[BIAS_ROW:P, :], ib[0:1, :])
+        nc.sync.dma_start(q_raw[:], qT[0].rearrange("(p j) n -> p j n", j=PACK))
+        scale_rows = k_scales[0].bitcast(I32)
+        for quad in range(4):
+            nc.sync.dma_start(scale_pool[32 * quad : 32 * quad + 4, :], scale_rows[4 * quad : 4 * quad + 4, :])
+        nc.sync.dma_start(word_pool[:], k_words[0].rearrange("p n t -> p (n t)").bitcast(I32))
+        nc.sync.dma_start(pos[:], ps[0].rearrange("(p c) o -> p (c o)", c=QB))
+
+        bias_row = sb.tile([P, N], F32, name="bias_row")
+        nc.vector.tensor_copy(bias_row[:], bias_pool[:].indirect(offsets[:]))
+        key_scales = sb.tile([P, N], U8, name="key_scales", align_bytes=64)
+        nc.vector.tensor_copy(key_scales[:], scale_pool[:].bitcast(U8).indirect(offsets[:]))
+
+        q_grouped = sb.tile([P, QB, P, PACK], BF16, name="q_grouped", align_bytes=64)
+        nc.scalar.activation(q_grouped[:], q_raw[:].rearrange("p j (m c) -> p c m j", c=QB), ACT.Copy)
+        q_codes = sb.tile([P, NQ], U32, name="q_codes", align_bytes=64)
+        q_scales = sb.tile([P, NQ], U8, name="q_scales", align_bytes=64)
+        nc.vector.quantize_mx(
+            out=q_codes[:].bitcast(FP8X4), scales=q_scales[:], in_=q_grouped[:].rearrange("p c m j -> p (c m j)")
+        )
+
+        turned = psum.tile([P, N // P, P], F32, name="turned")
+        for b in range(N // P):
+            nc.tensor.transpose(turned[:, b, :], bias_row[:, b * P : (b + 1) * P], ident[:])
+        bias_col = sb.tile([P, N // P], F32, name="bias_col")
+        nc.scalar.copy(bias_col[:], turned[:, :, BIAS_ROW])
+        spread = psum.tile([P, N], F32, name="spread")
+        for b in range(N // P):
+            nc.tensor.transpose(spread[:, b * P : (b + 1) * P], bias_col[:, b : b + 1].to_broadcast([P, P]), ident[:])
+        bias = sb.tile([P, N], F32, name="bias")
+        nc.scalar.copy(bias[:], spread[:])
+
+        chunks = []
+        for h in range(2):
+            slots = slice(h * HALF, (h + 1) * HALF)
+            keys = sb.tile([P, HALF], U32, name=f"keys{h}", align_bytes=64)
+            nc.vector.tensor_copy(
+                keys[:], word_pool[:].bitcast(U32).indirect(offsets[:, h * HALF // 16 : (h + 1) * HALF // 16])
+            )
+            for c in range(QB):
+                acc = psum.tile([P, HALF], F32, name=f"acc{h}{c}")
+                nc.tensor.matmul_mx(
+                    out=acc[:],
+                    lhsT=q_codes[:, c * P : (c + 1) * P].bitcast(FP8X4),
+                    lhsT_scale=q_scales[:, c * P : (c + 1) * P],
+                    rhs=keys[:].bitcast(FP8X4),
+                    rhs_scale=key_scales[:, slots],
+                    start=True,
+                    stop=True,
+                )
+                chunks.append((acc, c, slots, c * N + h * HALF))
+
+        for acc, c, slots, col in chunks:
+            nc.vector.scalar_tensor_tensor(
+                v[:, col : col + HALF], acc[:], pos[:, c : c + 1], bias[:, slots], ALU.subtract, ALU.add
+            )
+        for acc, c, slots, col in chunks:
+            end = col + HALF + (1 if col + HALF == QB * N else 0)
+            nc.scalar.activation(e[:, col:end], v[:, col:end], ACT.Exp)
+        for acc, c, slots, col in chunks:
+            nc.vector.tensor_scalar_min(e[:, col : col + HALF], e[:, col : col + HALF], EXP_CAP)
+        one = e[:, QB * N : QB * N + 1]
+        out_rows = out[0].rearrange("(p c) n -> p (c n)", c=QB)
+        for j in range(4):
+            cols = slice(j * HALF, (j + 1) * HALF)
+            nc.scalar.activation(lg[:, cols], e[:, cols], ACT.Ln, bias=one)
+            nc.vector.tensor_tensor(res[:, cols], lg[:, cols], v[:, cols], ALU.max)
+            nc.sync.dma_start(out_rows[:, cols], res[:, cols])

@@ -21,6 +21,8 @@ PACK = 4
 QB = NQ // P
 HALF = N // 2
 BIAS_ROW = P - 1
+ZERO_SPLIT = 1280
+TAIL = (320, 320, 256, 128)
 EXP_CAP = 2.0**60
 
 
@@ -32,7 +34,7 @@ def tile_attend_bpr_topk_kernel(tc, qT, k_words, k_scales, ib, ps, offs, out):
 
         offsets = sb.tile([P, N // 16], U16, name="offsets")
         bias_pool = sb.tile([P, T], F32, name="bias_pool")
-        scale_pool = sb.tile([P, T // 4], I32, name="scale_pool")
+        scale_pool = sb.tile([P, T // 4], I32, name="scale_pool", tag="scales_then_codes", align_bytes=64)
         word_pool = sb.tile([P, T], I32, name="word_pool")
         q_raw = sb.tile([P, PACK, NQ], F32, name="q_raw")
         pos = sb.tile([P, QB], F32, name="pos")
@@ -44,43 +46,54 @@ def tile_attend_bpr_topk_kernel(tc, qT, k_words, k_scales, ib, ps, offs, out):
         res = sb.tile([P, QB * N], F32, name="res")
 
         nc.vector.memset(scale_pool[:], 0)
-        nc.vector.memset(bias_pool[0:BIAS_ROW, :], 0.0)
-        nc.gpsimd.memset(zero[:], 0.0)
-        nc.scalar.activation(v[:, QB * N : QB * N + 1], zero[:], ACT.Copy)
+        nc.vector.memset(zero[:], 0.0)
+        nc.vector.memset(bias_pool[0:BIAS_ROW, 0:ZERO_SPLIT], 0.0)
+        nc.gpsimd.memset(bias_pool[0:BIAS_ROW, ZERO_SPLIT:T], 0.0)
         make_identity(nc, ident[:])
 
         nc.sync.dma_start(offsets[:], offs)
         nc.sync.dma_start(bias_pool[BIAS_ROW:P, :], ib[0:1, :])
         nc.sync.dma_start(q_raw[:], qT[0].rearrange("(p j) n -> p j n", j=PACK))
         scale_rows = k_scales[0].bitcast(I32)
-        for quad in range(4):
-            nc.sync.dma_start(scale_pool[32 * quad : 32 * quad + 4, :], scale_rows[4 * quad : 4 * quad + 4, :])
+        for r in range(4):
+            nc.sync.dma_start(scale_pool[r:P:32, :], scale_rows[r:16:4, :])
+        nc.scalar.activation(v[:, QB * N : QB * N + 1], zero[:], ACT.Copy)
         nc.sync.dma_start(word_pool[:], k_words[0].rearrange("p n t -> p (n t)").bitcast(I32))
         nc.sync.dma_start(pos[:], ps[0].rearrange("(p c) o -> p (c o)", c=QB))
 
         bias_row = sb.tile([P, N], F32, name="bias_row")
-        nc.vector.tensor_copy(bias_row[:], bias_pool[:].indirect(offsets[:]))
+        for h in range(2):
+            nc.vector.tensor_copy(
+                bias_row[:, h * HALF : (h + 1) * HALF],
+                bias_pool[:].indirect(offsets[:, h * HALF // 16 : (h + 1) * HALF // 16]),
+            )
         key_scales = sb.tile([P, N], U8, name="key_scales", align_bytes=64)
         nc.vector.tensor_copy(key_scales[:], scale_pool[:].bitcast(U8).indirect(offsets[:]))
 
         q_grouped = sb.tile([P, QB, P, PACK], BF16, name="q_grouped", align_bytes=64)
-        nc.scalar.activation(q_grouped[:], q_raw[:].rearrange("p j (m c) -> p c m j", c=QB), ACT.Copy)
-        q_codes = sb.tile([P, NQ], U32, name="q_codes", align_bytes=64)
+        q_src = q_raw[:].rearrange("p j (g i c) -> p c g j i", i=4, c=QB)
+        for c in range(QB):
+            nc.scalar.activation(q_grouped[:, c].rearrange("p (g i) j -> p g j i", i=4), q_src[:, c], ACT.Copy)
+        q_codes = sb.tile([P, NQ], U32, name="q_codes", tag="scales_then_codes", align_bytes=64)
         q_scales = sb.tile([P, NQ], U8, name="q_scales", align_bytes=64)
         nc.vector.quantize_mx(
             out=q_codes[:].bitcast(FP8X4), scales=q_scales[:], in_=q_grouped[:].rearrange("p c m j -> p (c m j)")
         )
 
-        turned = psum.tile([P, N // P, P], F32, name="turned")
-        for b in range(N // P):
-            nc.tensor.transpose(turned[:, b, :], bias_row[:, b * P : (b + 1) * P], ident[:])
-        bias_col = sb.tile([P, N // P], F32, name="bias_col")
-        nc.scalar.copy(bias_col[:], turned[:, :, BIAS_ROW])
-        spread = psum.tile([P, N], F32, name="spread")
-        for b in range(N // P):
-            nc.tensor.transpose(spread[:, b * P : (b + 1) * P], bias_col[:, b : b + 1].to_broadcast([P, P]), ident[:])
         bias = sb.tile([P, N], F32, name="bias")
-        nc.scalar.copy(bias[:], spread[:])
+        for h in range(2):
+            turned = psum.tile([P, HALF // P, P], F32, name=f"turned{h}")
+            for b in range(HALF // P):
+                first = h * HALF + b * P
+                nc.tensor.transpose(turned[:, b, :], bias_row[:, first : first + P], ident[:])
+            bias_col = sb.tile([P, HALF // P], F32, name=f"bias_col{h}")
+            nc.scalar.copy(bias_col[:], turned[:, :, BIAS_ROW])
+            spread = psum.tile([P, HALF], F32, name=f"spread{h}")
+            for b in range(HALF // P):
+                nc.tensor.transpose(
+                    spread[:, b * P : (b + 1) * P], bias_col[:, b : b + 1].to_broadcast([P, P]), ident[:]
+                )
+            nc.scalar.copy(bias[:, h * HALF : (h + 1) * HALF], spread[:])
 
         chunks = []
         for h in range(2):
@@ -109,12 +122,13 @@ def tile_attend_bpr_topk_kernel(tc, qT, k_words, k_scales, ib, ps, offs, out):
         for acc, c, slots, col in chunks:
             end = col + HALF + (1 if col + HALF == QB * N else 0)
             nc.scalar.activation(e[:, col:end], v[:, col:end], ACT.Exp)
-        for acc, c, slots, col in chunks:
-            nc.vector.tensor_scalar_min(e[:, col : col + HALF], e[:, col : col + HALF], EXP_CAP)
+        nc.vector.tensor_scalar_min(e[:, 0 : QB * N], e[:, 0 : QB * N], EXP_CAP)
         one = e[:, QB * N : QB * N + 1]
         out_rows = out[0].rearrange("(p c) n -> p (c n)", c=QB)
-        for j in range(4):
-            cols = slice(j * HALF, (j + 1) * HALF)
+        col = 0
+        for width in TAIL:
+            cols = slice(col, col + width)
+            col += width
             nc.scalar.activation(lg[:, cols], e[:, cols], ACT.Ln, bias=one)
             nc.vector.tensor_tensor(res[:, cols], lg[:, cols], v[:, cols], ALU.max)
             nc.sync.dma_start(out_rows[:, cols], res[:, cols])

@@ -22,7 +22,8 @@ QB = NQ // P
 HALF = N // 2
 BIAS_ROW = P - 1
 ZERO_SPLIT = 1280
-TAIL = (320, 320, 256, 128)
+STEP = 128
+STORES = (256, 256, 256, 128, 128)
 EXP_CAP = 2.0**60
 
 
@@ -125,10 +126,11 @@ def tile_attend_bpr_topk_kernel(tc, qT, k_words, k_scales, ib, ps, offs, out):
         nc.vector.tensor_scalar_min(e[:, 0 : QB * N], e[:, 0 : QB * N], EXP_CAP)
         one = e[:, QB * N : QB * N + 1]
         out_rows = out[0].rearrange("(p c) n -> p (c n)", c=QB)
-        col = 0
-        for width in TAIL:
-            cols = slice(col, col + width)
-            col += width
-            nc.scalar.activation(lg[:, cols], e[:, cols], ACT.Ln, bias=one)
-            nc.vector.tensor_tensor(res[:, cols], lg[:, cols], v[:, cols], ALU.max)
-            nc.sync.dma_start(out_rows[:, cols], res[:, cols])
+        first = 0
+        for width in STORES:
+            for col in range(first, first + width, STEP):
+                cols = slice(col, col + STEP)
+                nc.scalar.activation(lg[:, cols], e[:, cols], ACT.Ln, bias=one)
+                nc.vector.tensor_tensor(res[:, cols], lg[:, cols], v[:, cols], ALU.max)
+            nc.sync.dma_start(out_rows[:, first : first + width], res[:, first : first + width])
+            first += width

@@ -23,7 +23,7 @@ HALF = N // 2
 BIAS_ROW = P - 1
 ZERO_SPLIT = 1280
 STEP = 128
-STORES = (256, 256, 256, 128, 128)
+STORES = (128, 256, 256, 256, 128)
 EXP_CAP = 2.0**60
 
 
@@ -31,11 +31,12 @@ def tile_attend_bpr_topk_kernel(tc, qT, k_words, k_scales, ib, ps, offs, out):
     nc = tc.nc
     with ExitStack() as ctx:
         sb = ctx.enter_context(tc.tile_pool(name="sb", bufs=1))
+        reused = ctx.enter_context(tc.tile_pool(name="reused", bufs=1))
         psum = ctx.enter_context(tc.psum_pool(name="psum", bufs=1))
 
         offsets = sb.tile([P, N // 16], U16, name="offsets")
-        bias_pool = sb.tile([P, T], F32, name="bias_pool")
-        scale_pool = sb.tile([P, T // 4], I32, name="scale_pool", tag="scales_then_codes", align_bytes=64)
+        bias_pool = reused.tile([P, T], F32, name="bias_pool", align_bytes=64, offset=0)
+        scale_pool = sb.tile([P, T // 4], I32, name="scale_pool")
         word_pool = sb.tile([P, T], I32, name="word_pool")
         q_raw = sb.tile([P, PACK, NQ], F32, name="q_raw")
         pos = sb.tile([P, QB], F32, name="pos")
@@ -68,18 +69,23 @@ def tile_attend_bpr_topk_kernel(tc, qT, k_words, k_scales, ib, ps, offs, out):
                 bias_row[:, h * HALF : (h + 1) * HALF],
                 bias_pool[:].indirect(offsets[:, h * HALF // 16 : (h + 1) * HALF // 16]),
             )
-        key_scales = sb.tile([P, N], U8, name="key_scales", align_bytes=64)
-        nc.vector.tensor_copy(key_scales[:], scale_pool[:].bitcast(U8).indirect(offsets[:]))
 
-        q_grouped = sb.tile([P, QB, P, PACK], BF16, name="q_grouped", align_bytes=64)
+        q_even = sb.tile([P, P, PACK], BF16, name="q_even", align_bytes=64)
+        q_odd = reused.tile([P, P, PACK], BF16, name="q_odd", align_bytes=64, offset=0)
         q_src = q_raw[:].rearrange("p j (g i c) -> p c g j i", i=4, c=QB)
-        for c in range(QB):
-            nc.scalar.activation(q_grouped[:, c].rearrange("p (g i) j -> p g j i", i=4), q_src[:, c], ACT.Copy)
-        q_codes = sb.tile([P, NQ], U32, name="q_codes", tag="scales_then_codes", align_bytes=64)
+        nc.scalar.activation(q_even[:].rearrange("p (g i) j -> p g j i", i=4), q_src[:, 0], ACT.Copy)
+        nc.vector.tensor_copy(q_odd[:].rearrange("p (g i) j -> p g j i", i=4), q_src[:, 1])
+        q_codes = reused.tile([P, NQ], U32, name="q_codes", align_bytes=64, offset=2 * P * PACK)
         q_scales = sb.tile([P, NQ], U8, name="q_scales", align_bytes=64)
-        nc.vector.quantize_mx(
-            out=q_codes[:].bitcast(FP8X4), scales=q_scales[:], in_=q_grouped[:].rearrange("p c m j -> p (c m j)")
-        )
+        for c, grouped in enumerate((q_even, q_odd)):
+            nc.vector.quantize_mx(
+                out=q_codes[:, c * P : (c + 1) * P].bitcast(FP8X4),
+                scales=q_scales[:, c * P : (c + 1) * P],
+                in_=grouped[:].rearrange("p m j -> p (m j)"),
+            )
+
+        key_scales = reused.tile([P, N], U8, name="key_scales", align_bytes=64, offset=0)
+        nc.vector.tensor_copy(key_scales[:], scale_pool[:].bitcast(U8).indirect(offsets[:]))
 
         bias = sb.tile([P, N], F32, name="bias")
         for h in range(2):

@@ -21,7 +21,7 @@ PACK = 4
 QB = NQ // P
 HALF = N // 2
 BIAS_ROW = P - 1
-ZERO_SPLIT = 1280
+ZERO_SPLIT = 1536
 STEP = 128
 STORES = (128, 256, 256, 256, 128)
 EXP_CAP = 2.0**60
@@ -36,7 +36,7 @@ def tile_attend_bpr_topk_kernel(tc, qT, k_words, k_scales, ib, ps, offs, out):
 
         offsets = sb.tile([P, N // 16], U16, name="offsets")
         bias_pool = reused.tile([P, T], F32, name="bias_pool", align_bytes=64, offset=0)
-        scale_pool = sb.tile([P, T // 4], I32, name="scale_pool")
+        scale_pool = reused.tile([P, T // 4], I32, name="scale_pool", align_bytes=64, offset=5 * T)
         word_pool = sb.tile([P, T], I32, name="word_pool")
         q_raw = sb.tile([P, PACK, NQ], F32, name="q_raw")
         pos = sb.tile([P, QB], F32, name="pos")
@@ -47,9 +47,11 @@ def tile_attend_bpr_topk_kernel(tc, qT, k_words, k_scales, ib, ps, offs, out):
         lg = sb.tile([P, QB * N], F32, name="lg")
         res = sb.tile([P, QB * N], F32, name="res")
 
-        nc.vector.memset(scale_pool[:], 0)
+        nc.gpsimd.memset(scale_pool[:], 0)
         nc.vector.memset(zero[:], 0.0)
-        nc.vector.memset(bias_pool[0:BIAS_ROW, 0:ZERO_SPLIT], 0.0)
+        odd = ZERO_SPLIT // 2 - 1
+        nc.vector.memset(bias_pool[0:BIAS_ROW, 0:odd], 0.0)
+        nc.vector.memset(bias_pool[0:BIAS_ROW, odd:ZERO_SPLIT], 0.0)
         nc.gpsimd.memset(bias_pool[0:BIAS_ROW, ZERO_SPLIT:T], 0.0)
         make_identity(nc, ident[:])
 
@@ -70,22 +72,20 @@ def tile_attend_bpr_topk_kernel(tc, qT, k_words, k_scales, ib, ps, offs, out):
                 bias_pool[:].indirect(offsets[:, h * HALF // 16 : (h + 1) * HALF // 16]),
             )
 
-        q_even = sb.tile([P, P, PACK], BF16, name="q_even", align_bytes=64)
-        q_odd = reused.tile([P, P, PACK], BF16, name="q_odd", align_bytes=64, offset=0)
-        q_src = q_raw[:].rearrange("p j (g i c) -> p c g j i", i=4, c=QB)
-        nc.scalar.activation(q_even[:].rearrange("p (g i) j -> p g j i", i=4), q_src[:, 0], ACT.Copy)
-        nc.vector.tensor_copy(q_odd[:].rearrange("p (g i) j -> p g j i", i=4), q_src[:, 1])
-        q_codes = reused.tile([P, NQ], U32, name="q_codes", align_bytes=64, offset=2 * P * PACK)
-        q_scales = sb.tile([P, NQ], U8, name="q_scales", align_bytes=64)
-        for c, grouped in enumerate((q_even, q_odd)):
-            nc.vector.quantize_mx(
-                out=q_codes[:, c * P : (c + 1) * P].bitcast(FP8X4),
-                scales=q_scales[:, c * P : (c + 1) * P],
-                in_=grouped[:].rearrange("p m j -> p (m j)"),
-            )
-
         key_scales = reused.tile([P, N], U8, name="key_scales", align_bytes=64, offset=0)
         nc.vector.tensor_copy(key_scales[:], scale_pool[:].bitcast(U8).indirect(offsets[:]))
+
+        grouped = sb.tile([P, QB, P, PACK], BF16, name="grouped", align_bytes=64)
+        q_src = q_raw[:].rearrange("p j (g i c) -> p c g j i", i=4, c=QB)
+        for c in range(QB):
+            nc.scalar.activation(grouped[:, c].rearrange("p (g i) j -> p g j i", i=4), q_src[:, c], ACT.Copy)
+        q_codes = reused.tile([P, NQ], U32, name="q_codes", align_bytes=64, offset=5 * T)
+        q_scales = sb.tile([P, NQ], U8, name="q_scales", align_bytes=64)
+        nc.vector.quantize_mx(
+            out=q_codes[:].bitcast(FP8X4),
+            scales=q_scales[:],
+            in_=grouped[:].rearrange("p c m j -> p (c m j)"),
+        )
 
         bias = sb.tile([P, N], F32, name="bias")
         for h in range(2):

@@ -21,7 +21,7 @@ PACK = 4
 QB = NQ // P
 HALF = N // 2
 BIAS_ROW = P - 1
-ZERO_SPLIT = 1536
+ZERO_SPLIT = 1152
 STEP = 128
 STORES = (128, 256, 256, 256, 128)
 EXP_CAP = 2.0**60
@@ -72,7 +72,7 @@ def tile_attend_bpr_topk_kernel(tc, qT, k_words, k_scales, ib, ps, offs, out):
                 bias_pool[:].indirect(offsets[:, h * HALF // 16 : (h + 1) * HALF // 16]),
             )
 
-        key_scales = reused.tile([P, N], U8, name="key_scales", align_bytes=64, offset=0)
+        key_scales = sb.tile([P, N], U8, name="key_scales", align_bytes=64)
         nc.vector.tensor_copy(key_scales[:], scale_pool[:].bitcast(U8).indirect(offsets[:]))
 
         grouped = sb.tile([P, QB, P, PACK], BF16, name="grouped", align_bytes=64)

@@ -20,8 +20,11 @@ P = 128
 PACK = 4
 QB = NQ // P
 HALF = N // 2
+SB = N // P
 BIAS_ROW = P - 1
-ZERO_SPLIT = 1152
+SCALE_ROWS = 16
+SCALE_ROW0 = 48
+ZERO_SPLIT = 768
 STEP = 128
 STORES = (128, 256, 256, 256, 128)
 EXP_CAP = 2.0**60
@@ -36,50 +39,49 @@ def tile_attend_bpr_topk_kernel(tc, qT, k_words, k_scales, ib, ps, offs, out):
 
         offsets = sb.tile([P, N // 16], U16, name="offsets")
         bias_pool = reused.tile([P, T], F32, name="bias_pool", align_bytes=64, offset=0)
-        scale_pool = reused.tile([P, T // 4], I32, name="scale_pool", align_bytes=64, offset=5 * T)
+        scale_pool = reused.tile([P, T // 4], I32, name="scale_pool", align_bytes=64, offset=4 * T)
         word_pool = sb.tile([P, T], I32, name="word_pool")
-        q_raw = sb.tile([P, PACK, NQ], F32, name="q_raw")
+        q_raw = reused.tile([P, PACK, NQ], F32, name="q_raw", align_bytes=64, offset=5 * T)
         pos = sb.tile([P, QB], F32, name="pos")
-        zero = sb.tile([P, 1], F32, name="zero")
+        one = sb.tile([P, 1], F32, name="one")
         ident = sb.tile([P, P], F32, name="ident")
-        v = sb.tile([P, QB * N + 1], F32, name="v")
-        e = sb.tile([P, QB * N + 1], F32, name="e")
+        key_scales = sb.tile([P, N // 4], I32, name="key_scales", align_bytes=64)
+        v = sb.tile([P, QB * N], F32, name="v")
+        e = sb.tile([P, QB * N], F32, name="e")
         lg = sb.tile([P, QB * N], F32, name="lg")
         res = sb.tile([P, QB * N], F32, name="res")
 
-        nc.gpsimd.memset(scale_pool[:], 0)
-        nc.vector.memset(zero[:], 0.0)
+        nc.sync.dma_start(offsets[:], offs)
+        nc.scalar.dma_start(scale_pool[SCALE_ROW0 : SCALE_ROW0 + SCALE_ROWS, :], k_scales[0].bitcast(I32))
+        nc.sync.dma_start(q_raw[:], qT[0].rearrange("(p j) n -> p j n", j=PACK))
+        nc.scalar.dma_start(bias_pool[BIAS_ROW:P, :], ib[0:1, :])
+        nc.sync.dma_start(pos[:], ps[0].rearrange("(p c) o -> p (c o)", c=QB))
+        nc.sync.dma_start(word_pool[:], k_words[0].rearrange("p n t -> p (n t)").bitcast(I32))
+
+        nc.vector.memset(scale_pool[0:SCALE_ROW0, :], 0)
+        nc.vector.memset(scale_pool[SCALE_ROW0 + SCALE_ROWS : P, :], 0)
         odd = ZERO_SPLIT // 2 - 1
         nc.vector.memset(bias_pool[0:BIAS_ROW, 0:odd], 0.0)
         nc.vector.memset(bias_pool[0:BIAS_ROW, odd:ZERO_SPLIT], 0.0)
         nc.gpsimd.memset(bias_pool[0:BIAS_ROW, ZERO_SPLIT:T], 0.0)
+        nc.gpsimd.memset(key_scales[:], 0)
+        nc.gpsimd.memset(one[:], 1.0)
         make_identity(nc, ident[:])
 
-        nc.sync.dma_start(offsets[:], offs)
-        nc.sync.dma_start(bias_pool[BIAS_ROW:P, :], ib[0:1, :])
-        nc.sync.dma_start(q_raw[:], qT[0].rearrange("(p j) n -> p j n", j=PACK))
-        scale_rows = k_scales[0].bitcast(I32)
+        picked_scales = sb.tile([P, N], U8, name="picked_scales", align_bytes=64)
+        nc.vector.tensor_copy(picked_scales[:], scale_pool[:].bitcast(U8).indirect(offsets[:]))
+        picked_rows = picked_scales[:].bitcast(I32)
         for r in range(4):
-            nc.sync.dma_start(scale_pool[r:P:32, :], scale_rows[r:16:4, :])
-        nc.scalar.activation(v[:, QB * N : QB * N + 1], zero[:], ACT.Copy)
-        nc.sync.dma_start(word_pool[:], k_words[0].rearrange("p n t -> p (n t)").bitcast(I32))
-        nc.sync.dma_start(pos[:], ps[0].rearrange("(p c) o -> p (c o)", c=QB))
+            nc.sync.dma_start(key_scales[r:P:32, :], picked_rows[SCALE_ROW0 + r : SCALE_ROW0 + SCALE_ROWS : 4, :])
 
         bias_row = sb.tile([P, N], F32, name="bias_row")
-        for h in range(2):
-            nc.vector.tensor_copy(
-                bias_row[:, h * HALF : (h + 1) * HALF],
-                bias_pool[:].indirect(offsets[:, h * HALF // 16 : (h + 1) * HALF // 16]),
-            )
-
-        key_scales = sb.tile([P, N], U8, name="key_scales", align_bytes=64)
-        nc.vector.tensor_copy(key_scales[:], scale_pool[:].bitcast(U8).indirect(offsets[:]))
+        nc.vector.tensor_copy(bias_row[:], bias_pool[:].indirect(offsets[:]))
 
         grouped = sb.tile([P, QB, P, PACK], BF16, name="grouped", align_bytes=64)
         q_src = q_raw[:].rearrange("p j (g i c) -> p c g j i", i=4, c=QB)
         for c in range(QB):
             nc.scalar.activation(grouped[:, c].rearrange("p (g i) j -> p g j i", i=4), q_src[:, c], ACT.Copy)
-        q_codes = reused.tile([P, NQ], U32, name="q_codes", align_bytes=64, offset=5 * T)
+        q_codes = reused.tile([P, NQ], U32, name="q_codes", align_bytes=64, offset=0)
         q_scales = sb.tile([P, NQ], U8, name="q_scales", align_bytes=64)
         nc.vector.quantize_mx(
             out=q_codes[:].bitcast(FP8X4),
@@ -87,56 +89,69 @@ def tile_attend_bpr_topk_kernel(tc, qT, k_words, k_scales, ib, ps, offs, out):
             in_=grouped[:].rearrange("p c m j -> p (c m j)"),
         )
 
-        bias = sb.tile([P, N], F32, name="bias")
-        for h in range(2):
-            turned = psum.tile([P, HALF // P, P], F32, name=f"turned{h}")
-            for b in range(HALF // P):
-                first = h * HALF + b * P
-                nc.tensor.transpose(turned[:, b, :], bias_row[:, first : first + P], ident[:])
-            bias_col = sb.tile([P, HALF // P], F32, name=f"bias_col{h}")
-            nc.scalar.copy(bias_col[:], turned[:, :, BIAS_ROW])
-            spread = psum.tile([P, HALF], F32, name=f"spread{h}")
-            for b in range(HALF // P):
-                nc.tensor.transpose(
-                    spread[:, b * P : (b + 1) * P], bias_col[:, b : b + 1].to_broadcast([P, P]), ident[:]
-                )
-            nc.scalar.copy(bias[:, h * HALF : (h + 1) * HALF], spread[:])
+        pos_spread = psum.tile([P, NQ], F32, name="exp_bank0")
+        for c in range(QB):
+            nc.tensor.transpose(pos_spread[:, c * P : (c + 1) * P], pos[:, c : c + 1].to_broadcast([P, P]), ident[:])
+        pos_row = reused.tile([P, NQ], F32, name="pos_row", align_bytes=64, offset=5 * T)
+        nc.scalar.copy(pos_row[:], pos_spread[:])
 
-        chunks = []
+        bias_cols = []
+        for b in range(SB):
+            turned = psum.tile([P, P], F32, name=f"bank{b}")
+            nc.tensor.transpose(turned[:], bias_row[:, b * P : (b + 1) * P], ident[:])
+            bias_col = sb.tile([P, 1], F32, name=f"bias_col{b}")
+            nc.scalar.copy(bias_col[:], turned[:, BIAS_ROW:P])
+            bias_cols.append(bias_col)
+
+        scores = []
         for h in range(2):
-            slots = slice(h * HALF, (h + 1) * HALF)
-            keys = sb.tile([P, HALF], U32, name=f"keys{h}", align_bytes=64)
+            keys = reused.tile([P, HALF], U32, name=f"keys{h}", align_bytes=64, offset=4 * NQ + 4 * HALF * h)
             nc.vector.tensor_copy(
                 keys[:], word_pool[:].bitcast(U32).indirect(offsets[:, h * HALF // 16 : (h + 1) * HALF // 16])
             )
-            for c in range(QB):
-                acc = psum.tile([P, HALF], F32, name=f"acc{h}{c}")
+            for k in range(HALF // P):
+                b = h * (HALF // P) + k
+                acc = psum.tile([P, NQ], F32, name=f"bank{b}")
                 nc.tensor.matmul_mx(
                     out=acc[:],
-                    lhsT=q_codes[:, c * P : (c + 1) * P].bitcast(FP8X4),
-                    lhsT_scale=q_scales[:, c * P : (c + 1) * P],
-                    rhs=keys[:].bitcast(FP8X4),
-                    rhs_scale=key_scales[:, slots],
+                    lhsT=keys[:, k * P : (k + 1) * P].bitcast(FP8X4),
+                    lhsT_scale=key_scales[:].bitcast(U8)[:, b * P : (b + 1) * P],
+                    rhs=q_codes[:].bitcast(FP8X4),
+                    rhs_scale=q_scales[:],
                     start=True,
                     stop=True,
                 )
-                chunks.append((acc, c, slots, c * N + h * HALF))
+                scores.append(acc)
 
-        for acc, c, slots, col in chunks:
+        for b in range(SB):
             nc.vector.scalar_tensor_tensor(
-                v[:, col : col + HALF], acc[:], pos[:, c : c + 1], bias[:, slots], ALU.subtract, ALU.add
+                v[:, b * NQ : (b + 1) * NQ], scores[b][:], bias_cols[b][:], pos_row[:], ALU.add, ALU.subtract
             )
-        for acc, c, slots, col in chunks:
-            end = col + HALF + (1 if col + HALF == QB * N else 0)
-            nc.scalar.activation(e[:, col:end], v[:, col:end], ACT.Exp)
-        nc.vector.tensor_scalar_min(e[:, 0 : QB * N], e[:, 0 : QB * N], EXP_CAP)
-        one = e[:, QB * N : QB * N + 1]
+        for b in range(SB):
+            nc.scalar.activation(e[:, b * NQ : (b + 1) * NQ], v[:, b * NQ : (b + 1) * NQ], ACT.Exp)
+        capped = reused.tile([P, QB * N], F32, name="capped", align_bytes=64, offset=5 * T)
+        for b in range(SB):
+            nc.vector.tensor_scalar_min(capped[:, b * NQ : (b + 1) * NQ], e[:, b * NQ : (b + 1) * NQ], EXP_CAP)
+
+        v_rows = []
+        e_rows = []
+        for c in range(QB):
+            v_bank = psum.tile([P, N], F32, name=f"margin_bank{c}")
+            e_bank = psum.tile([P, N], F32, name=f"exp_bank{c}")
+            for b in range(SB):
+                cols = slice(b * NQ + c * P, b * NQ + (c + 1) * P)
+                nc.tensor.transpose(e_bank[:, b * P : (b + 1) * P], capped[:, cols], ident[:])
+                nc.tensor.transpose(v_bank[:, b * P : (b + 1) * P], v[:, cols], ident[:])
+            v_rows.append(v_bank)
+            e_rows.append(e_bank)
+
         out_rows = out[0].rearrange("(p c) n -> p (c n)", c=QB)
         first = 0
         for width in STORES:
             for col in range(first, first + width, STEP):
+                c, slot = divmod(col, N)
                 cols = slice(col, col + STEP)
-                nc.scalar.activation(lg[:, cols], e[:, cols], ACT.Ln, bias=one)
-                nc.vector.tensor_tensor(res[:, cols], lg[:, cols], v[:, cols], ALU.max)
+                nc.scalar.activation(lg[:, cols], e_rows[c][:, slot : slot + STEP], ACT.Ln, bias=one[:])
+                nc.vector.tensor_tensor(res[:, cols], lg[:, cols], v_rows[c][:, slot : slot + STEP], ALU.max)
             nc.sync.dma_start(out_rows[:, first : first + width], res[:, first : first + width])
             first += width

@@ -58,8 +58,9 @@ def tile_attend_bpr_topk_kernel(tc, qT, k_words, k_scales, ib, ps, offs, out):
         nc.sync.dma_start(pos[:], ps[0].rearrange("(p c) o -> p (c o)", c=QB))
         nc.sync.dma_start(word_pool[:], k_words[0].rearrange("p n t -> p (n t)").bitcast(I32))
 
-        nc.vector.memset(scale_pool[0:SCALE_ROW0, :], 0)
-        nc.vector.memset(scale_pool[SCALE_ROW0 + SCALE_ROWS : P, :], 0)
+        for rows in (slice(0, SCALE_ROW0), slice(SCALE_ROW0 + SCALE_ROWS, P)):
+            nc.vector.memset(scale_pool[rows, 0 : T // 8 - 1], 0)
+            nc.vector.memset(scale_pool[rows, T // 8 - 1 : T // 4], 0)
         odd = ZERO_SPLIT // 2 - 1
         nc.vector.memset(bias_pool[0:BIAS_ROW, 0:odd], 0.0)
         nc.vector.memset(bias_pool[0:BIAS_ROW, odd:ZERO_SPLIT], 0.0)

@@ -24,7 +24,7 @@ SB = N // P
 BIAS_ROW = P - 1
 SCALE_ROWS = 16
 SCALE_ROW0 = 48
-ZERO_SPLIT = 768
+ZERO_SPLIT = 256
 STEP = 128
 STORES = (128, 256, 256, 256, 128)
 EXP_CAP = 2.0**60
@@ -42,7 +42,7 @@ def tile_attend_bpr_topk_kernel(tc, qT, k_words, k_scales, ib, ps, offs, out):
         scale_pool = reused.tile([P, T // 4], I32, name="scale_pool", align_bytes=64, offset=4 * T)
         word_pool = sb.tile([P, T], I32, name="word_pool")
         q_raw = reused.tile([P, PACK, NQ], F32, name="q_raw", align_bytes=64, offset=5 * T)
-        pos = sb.tile([P, QB], F32, name="pos")
+        pos = reused.tile([P, 32], F32, name="pos", align_bytes=64, offset=8 * T - 64)
         one = sb.tile([P, 1], F32, name="one")
         ident = sb.tile([P, P], F32, name="ident")
         key_scales = sb.tile([P, N // 4], I32, name="key_scales", align_bytes=64)
@@ -55,7 +55,7 @@ def tile_attend_bpr_topk_kernel(tc, qT, k_words, k_scales, ib, ps, offs, out):
         nc.scalar.dma_start(scale_pool[SCALE_ROW0 : SCALE_ROW0 + SCALE_ROWS, :], k_scales[0].bitcast(I32))
         nc.sync.dma_start(q_raw[:], qT[0].rearrange("(p j) n -> p j n", j=PACK))
         nc.scalar.dma_start(bias_pool[BIAS_ROW:P, :], ib[0:1, :])
-        nc.sync.dma_start(pos[:], ps[0].rearrange("(p c) o -> p (c o)", c=QB))
+        nc.sync.dma_start(pos[:, 0:QB], ps[0].rearrange("(p c) o -> p (c o)", c=QB))
         nc.sync.dma_start(word_pool[:], k_words[0].rearrange("p n t -> p (n t)").bitcast(I32))
 
         for rows in (slice(0, SCALE_ROW0), slice(SCALE_ROW0 + SCALE_ROWS, P)):
@@ -82,7 +82,7 @@ def tile_attend_bpr_topk_kernel(tc, qT, k_words, k_scales, ib, ps, offs, out):
         q_src = q_raw[:].rearrange("p j (g i c) -> p c g j i", i=4, c=QB)
         for c in range(QB):
             nc.scalar.activation(grouped[:, c].rearrange("p (g i) j -> p g j i", i=4), q_src[:, c], ACT.Copy)
-        q_codes = reused.tile([P, NQ], U32, name="q_codes", align_bytes=64, offset=0)
+        q_codes = reused.tile([P, NQ], U32, name="q_codes", align_bytes=64, offset=8 * T - 4 * NQ)
         q_scales = sb.tile([P, NQ], U8, name="q_scales", align_bytes=64)
         nc.vector.quantize_mx(
             out=q_codes[:].bitcast(FP8X4),
@@ -105,17 +105,17 @@ def tile_attend_bpr_topk_kernel(tc, qT, k_words, k_scales, ib, ps, offs, out):
             bias_cols.append(bias_col)
 
         scores = []
+        keys = reused.tile([P, N], U32, name="keys", align_bytes=64, offset=8 * T)
         for h in range(2):
-            keys = reused.tile([P, HALF], U32, name=f"keys{h}", align_bytes=64, offset=4 * NQ + 4 * HALF * h)
             nc.vector.tensor_copy(
-                keys[:], word_pool[:].bitcast(U32).indirect(offsets[:, h * HALF // 16 : (h + 1) * HALF // 16])
+                keys[:, h * HALF : (h + 1) * HALF], word_pool[:].bitcast(U32).indirect(offsets[:, h * HALF // 16 : (h + 1) * HALF // 16])
             )
             for k in range(HALF // P):
                 b = h * (HALF // P) + k
                 acc = psum.tile([P, NQ], F32, name=f"bank{b}")
                 nc.tensor.matmul_mx(
                     out=acc[:],
-                    lhsT=keys[:, k * P : (k + 1) * P].bitcast(FP8X4),
+                    lhsT=keys[:, b * P : (b + 1) * P].bitcast(FP8X4),
                     lhsT_scale=key_scales[:].bitcast(U8)[:, b * P : (b + 1) * P],
                     rhs=q_codes[:].bitcast(FP8X4),
                     rhs_scale=q_scales[:],

@@ -25,6 +25,7 @@ BIAS_ROW = P - 1
 SCALE_ROWS = 16
 SCALE_ROW0 = 48
 ZERO_SPLIT = 256
+SECOND_BANK = ("exp_bank0", "margin_bank0", "margin_bank1", "exp_bank1")
 STEP = 128
 STORES = (128, 256, 256, 256, 128)
 EXP_CAP = 2.0**60
@@ -42,7 +43,7 @@ def tile_attend_bpr_topk_kernel(tc, qT, k_words, k_scales, ib, ps, offs, out):
         scale_pool = reused.tile([P, T // 4], I32, name="scale_pool", align_bytes=64, offset=4 * T)
         word_pool = sb.tile([P, T], I32, name="word_pool")
         q_raw = reused.tile([P, PACK, NQ], F32, name="q_raw", align_bytes=64, offset=5 * T)
-        pos = reused.tile([P, 32], F32, name="pos", align_bytes=64, offset=8 * T - 64)
+        pos = reused.tile([P, 32 + N // 4], F32, name="pos", align_bytes=64, offset=8 * T - 64)
         one = sb.tile([P, 1], F32, name="one")
         ident = sb.tile([P, P], F32, name="ident")
         key_scales = sb.tile([P, N // 4], I32, name="key_scales", align_bytes=64)
@@ -105,31 +106,36 @@ def tile_attend_bpr_topk_kernel(tc, qT, k_words, k_scales, ib, ps, offs, out):
             bias_cols.append(bias_col)
 
         scores = []
-        keys = reused.tile([P, N], U32, name="keys", align_bytes=64, offset=8 * T)
+        plane = reused.tile([P, N // 4], I32, name="plane", align_bytes=64, offset=8 * T)
+        keys = reused.tile([P, N], U32, name="keys", align_bytes=64, offset=8 * T + N)
         for h in range(2):
             nc.vector.tensor_copy(
                 keys[:, h * HALF : (h + 1) * HALF], word_pool[:].bitcast(U32).indirect(offsets[:, h * HALF // 16 : (h + 1) * HALF // 16])
             )
-            for k in range(HALF // P):
-                b = h * (HALF // P) + k
-                acc = psum.tile([P, NQ], F32, name=f"bank{b}")
-                nc.tensor.matmul_mx(
-                    out=acc[:],
-                    lhsT=keys[:, b * P : (b + 1) * P].bitcast(FP8X4),
-                    lhsT_scale=key_scales[:].bitcast(U8)[:, b * P : (b + 1) * P],
-                    rhs=q_codes[:].bitcast(FP8X4),
-                    rhs_scale=q_scales[:],
-                    start=True,
-                    stop=True,
-                )
-                scores.append(acc)
+            if h == 0:
+                nc.vector.tensor_copy(plane[:], key_scales[:])
+            for b in range(h * SB // 2, (h + 1) * SB // 2):
+                width = P
+                for first in range(0, NQ, width):
+                    acc = psum.tile([P, width], F32, name=SECOND_BANK[b] if first else f"bank{b}")
+                    queries = slice(first, first + width)
+                    nc.tensor.matmul_mx(
+                        out=acc[:],
+                        lhsT=keys[:, b * P : (b + 1) * P].bitcast(FP8X4),
+                        lhsT_scale=plane[:].bitcast(U8)[:, b * P : (b + 1) * P],
+                        rhs=q_codes[:, queries].bitcast(FP8X4),
+                        rhs_scale=q_scales[:, queries],
+                        start=True,
+                        stop=True,
+                    )
+                    scores.append((acc, b, queries, slice(b * NQ + first, b * NQ + first + width)))
 
-        for b in range(SB):
+        for acc, b, queries, cols in scores:
             nc.vector.scalar_tensor_tensor(
-                v[:, b * NQ : (b + 1) * NQ], scores[b][:], bias_cols[b][:], pos_row[:], ALU.add, ALU.subtract
+                v[:, cols], acc[:], bias_cols[b][:], pos_row[:, queries], ALU.add, ALU.subtract
             )
-        for b in range(SB):
-            nc.scalar.activation(e[:, b * NQ : (b + 1) * NQ], v[:, b * NQ : (b + 1) * NQ], ACT.Exp)
+        for acc, b, queries, cols in scores:
+            nc.scalar.activation(e[:, cols], v[:, cols], ACT.Exp)
         capped = reused.tile([P, QB * N], F32, name="capped", align_bytes=64, offset=5 * T)
         for b in range(SB):
             nc.vector.tensor_scalar_min(capped[:, b * NQ : (b + 1) * NQ], e[:, b * NQ : (b + 1) * NQ], EXP_CAP)

@@ -19,15 +19,14 @@ ALU = mybir.AluOpType
 P = 128
 PACK = 4
 QB = NQ // P
-HALF = N // 2
 SB = N // P
 BIAS_ROW = P - 1
+HALF = N // 2
 SCALE_ROWS = 16
 SCALE_ROW0 = 48
 ZERO_SPLIT = 256
-SECOND_BANK = ("exp_bank0", "margin_bank0", "margin_bank1", "exp_bank1")
 STEP = 128
-STORES = (128, 256, 256, 256, 128)
+STORES = (128, 128, 256, 256, 256)
 EXP_CAP = 2.0**60
 
 
@@ -40,24 +39,29 @@ def tile_attend_bpr_topk_kernel(tc, qT, k_words, k_scales, ib, ps, offs, out):
 
         offsets = sb.tile([P, N // 16], U16, name="offsets")
         bias_pool = reused.tile([P, T], F32, name="bias_pool", align_bytes=64, offset=0)
-        scale_pool = reused.tile([P, T // 4], I32, name="scale_pool", align_bytes=64, offset=4 * T)
+        scale_pool = sb.tile([P, T // 4], I32, name="scale_pool", align_bytes=64)
         word_pool = sb.tile([P, T], I32, name="word_pool")
-        q_raw = reused.tile([P, PACK, NQ], F32, name="q_raw", align_bytes=64, offset=5 * T)
-        pos = reused.tile([P, 32 + N // 4], F32, name="pos", align_bytes=64, offset=8 * T - 64)
+        q_raw = [sb.tile([P, PACK, P], F32, name=f"q_raw{c}", align_bytes=64) for c in range(QB)]
+        pos_pairs = sb.tile([P, 2], F32, name="pos_pairs")
         one = sb.tile([P, 1], F32, name="one")
         ident = sb.tile([P, P], F32, name="ident")
         key_scales = sb.tile([P, N // 4], I32, name="key_scales", align_bytes=64)
         v = sb.tile([P, QB * N], F32, name="v")
         e = sb.tile([P, QB * N], F32, name="e")
+        capped = sb.tile([P, QB * N], F32, name="capped")
         lg = sb.tile([P, QB * N], F32, name="lg")
         res = sb.tile([P, QB * N], F32, name="res")
 
+        def load_queries(c):
+            nc.sync.dma_start(q_raw[c][:], qT[0, :, c * P : (c + 1) * P].rearrange("(p j) n -> p j n", j=PACK))
+
         nc.sync.dma_start(offsets[:], offs)
         nc.scalar.dma_start(scale_pool[SCALE_ROW0 : SCALE_ROW0 + SCALE_ROWS, :], k_scales[0].bitcast(I32))
-        nc.sync.dma_start(q_raw[:], qT[0].rearrange("(p j) n -> p j n", j=PACK))
+        load_queries(0)
         nc.scalar.dma_start(bias_pool[BIAS_ROW:P, :], ib[0:1, :])
-        nc.sync.dma_start(pos[:, 0:QB], ps[0].rearrange("(p c) o -> p (c o)", c=QB))
+        nc.sync.dma_start(pos_pairs[:], ps[0].rearrange("(p i) o -> p (i o)", i=2))
         nc.sync.dma_start(word_pool[:], k_words[0].rearrange("p n t -> p (n t)").bitcast(I32))
+        load_queries(1)
 
         for rows in (slice(0, SCALE_ROW0), slice(SCALE_ROW0 + SCALE_ROWS, P)):
             nc.vector.memset(scale_pool[rows, 0 : T // 8 - 1], 0)
@@ -65,37 +69,50 @@ def tile_attend_bpr_topk_kernel(tc, qT, k_words, k_scales, ib, ps, offs, out):
         odd = ZERO_SPLIT // 2 - 1
         nc.vector.memset(bias_pool[0:BIAS_ROW, 0:odd], 0.0)
         nc.vector.memset(bias_pool[0:BIAS_ROW, odd:ZERO_SPLIT], 0.0)
-        nc.gpsimd.memset(bias_pool[0:BIAS_ROW, ZERO_SPLIT:T], 0.0)
-        nc.gpsimd.memset(key_scales[:], 0)
         nc.gpsimd.memset(one[:], 1.0)
         make_identity(nc, ident[:])
+        nc.gpsimd.memset(bias_pool[0:BIAS_ROW, ZERO_SPLIT:T], 0.0)
+        nc.gpsimd.memset(key_scales[:], 0)
 
         picked_scales = sb.tile([P, N], U8, name="picked_scales", align_bytes=64)
         nc.vector.tensor_copy(picked_scales[:], scale_pool[:].bitcast(U8).indirect(offsets[:]))
         picked_rows = picked_scales[:].bitcast(I32)
         for r in range(4):
             nc.sync.dma_start(key_scales[r:P:32, :], picked_rows[SCALE_ROW0 + r : SCALE_ROW0 + SCALE_ROWS : 4, :])
-
-        bias_row = sb.tile([P, N], F32, name="bias_row")
+        bias_row = reused.tile([P, N], F32, name="bias_row", align_bytes=64, offset=4 * T)
         nc.vector.tensor_copy(bias_row[:], bias_pool[:].indirect(offsets[:]))
 
-        grouped = sb.tile([P, QB, P, PACK], BF16, name="grouped", align_bytes=64)
-        q_src = q_raw[:].rearrange("p j (g i c) -> p c g j i", i=4, c=QB)
-        for c in range(QB):
-            nc.scalar.activation(grouped[:, c].rearrange("p (g i) j -> p g j i", i=4), q_src[:, c], ACT.Copy)
-        q_codes = reused.tile([P, NQ], U32, name="q_codes", align_bytes=64, offset=8 * T - 4 * NQ)
+        grouped = [
+            sb.tile([P, P, PACK], BF16, name="grouped0", align_bytes=64),
+            reused.tile([P, P, PACK], BF16, name="grouped1", align_bytes=64, offset=4 * T),
+        ]
+        q_codes = reused.tile([P, NQ], U32, name="q_codes", align_bytes=64, offset=0)
         q_scales = sb.tile([P, NQ], U8, name="q_scales", align_bytes=64)
-        nc.vector.quantize_mx(
-            out=q_codes[:].bitcast(FP8X4),
-            scales=q_scales[:],
-            in_=grouped[:].rearrange("p c m j -> p (c m j)"),
-        )
+        keys = reused.tile([P, N], U32, name="keys", align_bytes=64, offset=4 * NQ)
 
-        pos_spread = psum.tile([P, NQ], F32, name="exp_bank0")
+        def quantise(c):
+            nc.scalar.activation(
+                grouped[c][:].rearrange("p (g i) j -> p g j i", i=4),
+                q_raw[c][:].rearrange("p j (g i) -> p g j i", i=4),
+                ACT.Copy,
+            )
+            nc.vector.quantize_mx(
+                out=q_codes[:, c * P : (c + 1) * P].bitcast(FP8X4),
+                scales=q_scales[:, c * P : (c + 1) * P],
+                in_=grouped[c][:].rearrange("p m j -> p (m j)"),
+            )
+
+        quantise(0)
+
+        pos_spread = psum.tile([P, 2, P], F32, name="bank4")
+        for i in range(2):
+            nc.tensor.transpose(pos_spread[:, i], pos_pairs[:, i : i + 1].to_broadcast([P, P]), ident[:])
+        pos_row = sb.tile([P, NQ], F32, name="pos_row")
         for c in range(QB):
-            nc.tensor.transpose(pos_spread[:, c * P : (c + 1) * P], pos[:, c : c + 1].to_broadcast([P, P]), ident[:])
-        pos_row = reused.tile([P, NQ], F32, name="pos_row", align_bytes=64, offset=5 * T)
-        nc.scalar.copy(pos_row[:], pos_spread[:])
+            nc.scalar.copy(
+                pos_row[:, c * P : (c + 1) * P].rearrange("p (n i) -> p n i", i=2),
+                pos_spread[:, :, c * P // 2 : (c + 1) * P // 2].rearrange("p i n -> p n i"),
+            )
 
         bias_cols = []
         for b in range(SB):
@@ -105,30 +122,28 @@ def tile_attend_bpr_topk_kernel(tc, qT, k_words, k_scales, ib, ps, offs, out):
             nc.scalar.copy(bias_col[:], turned[:, BIAS_ROW:P])
             bias_cols.append(bias_col)
 
-        scores = []
-        plane = reused.tile([P, N // 4], I32, name="plane", align_bytes=64, offset=8 * T)
-        keys = reused.tile([P, N], U32, name="keys", align_bytes=64, offset=8 * T + N)
         for h in range(2):
             nc.vector.tensor_copy(
-                keys[:, h * HALF : (h + 1) * HALF], word_pool[:].bitcast(U32).indirect(offsets[:, h * HALF // 16 : (h + 1) * HALF // 16])
+                keys[:, h * HALF : (h + 1) * HALF],
+                word_pool[:].bitcast(U32).indirect(offsets[:, h * HALF // 16 : (h + 1) * HALF // 16]),
             )
-            if h == 0:
-                nc.vector.tensor_copy(plane[:], key_scales[:])
-            for b in range(h * SB // 2, (h + 1) * SB // 2):
-                width = P
-                for first in range(0, NQ, width):
-                    acc = psum.tile([P, width], F32, name=SECOND_BANK[b] if first else f"bank{b}")
-                    queries = slice(first, first + width)
-                    nc.tensor.matmul_mx(
-                        out=acc[:],
-                        lhsT=keys[:, b * P : (b + 1) * P].bitcast(FP8X4),
-                        lhsT_scale=plane[:].bitcast(U8)[:, b * P : (b + 1) * P],
-                        rhs=q_codes[:, queries].bitcast(FP8X4),
-                        rhs_scale=q_scales[:, queries],
-                        start=True,
-                        stop=True,
-                    )
-                    scores.append((acc, b, queries, slice(b * NQ + first, b * NQ + first + width)))
+        quantise(1)
+
+        scores = []
+        for c in range(QB):
+            queries = slice(c * P, (c + 1) * P)
+            for b in range(SB):
+                acc = psum.tile([P, P], F32, name=f"bank{c * SB + b}")
+                nc.tensor.matmul_mx(
+                    out=acc[:],
+                    lhsT=keys[:, b * P : (b + 1) * P].bitcast(FP8X4),
+                    lhsT_scale=key_scales[:].bitcast(U8)[:, b * P : (b + 1) * P],
+                    rhs=q_codes[:, queries].bitcast(FP8X4),
+                    rhs_scale=q_scales[:, queries],
+                    start=True,
+                    stop=True,
+                )
+                scores.append((acc, b, queries, slice(c * N + b * P, c * N + (b + 1) * P)))
 
         for acc, b, queries, cols in scores:
             nc.vector.scalar_tensor_tensor(
@@ -136,29 +151,27 @@ def tile_attend_bpr_topk_kernel(tc, qT, k_words, k_scales, ib, ps, offs, out):
             )
         for acc, b, queries, cols in scores:
             nc.scalar.activation(e[:, cols], v[:, cols], ACT.Exp)
-        capped = reused.tile([P, QB * N], F32, name="capped", align_bytes=64, offset=5 * T)
-        for b in range(SB):
-            nc.vector.tensor_scalar_min(capped[:, b * NQ : (b + 1) * NQ], e[:, b * NQ : (b + 1) * NQ], EXP_CAP)
 
         v_rows = []
+        for c in range(QB):
+            v_bank = psum.tile([P, N], F32, name=f"bank{c}")
+            for b in range(SB):
+                nc.tensor.transpose(v_bank[:, b * P : (b + 1) * P], v[:, c * N + b * P : c * N + (b + 1) * P], ident[:])
+            v_rows.append(v_bank)
         e_rows = []
         for c in range(QB):
-            v_bank = psum.tile([P, N], F32, name=f"margin_bank{c}")
-            e_bank = psum.tile([P, N], F32, name=f"exp_bank{c}")
+            nc.vector.tensor_scalar_min(capped[:, c * N : (c + 1) * N], e[:, c * N : (c + 1) * N], EXP_CAP)
+            e_bank = psum.tile([P, N], F32, name=f"bank{QB + c}")
             for b in range(SB):
-                cols = slice(b * NQ + c * P, b * NQ + (c + 1) * P)
-                nc.tensor.transpose(e_bank[:, b * P : (b + 1) * P], capped[:, cols], ident[:])
-                nc.tensor.transpose(v_bank[:, b * P : (b + 1) * P], v[:, cols], ident[:])
-            v_rows.append(v_bank)
+                nc.tensor.transpose(e_bank[:, b * P : (b + 1) * P], capped[:, c * N + b * P : c * N + (b + 1) * P], ident[:])
             e_rows.append(e_bank)
 
-        out_rows = out[0].rearrange("(p c) n -> p (c n)", c=QB)
         first = 0
         for width in STORES:
-            for col in range(first, first + width, STEP):
-                c, slot = divmod(col, N)
-                cols = slice(col, col + STEP)
+            c, start = divmod(first, N)
+            for slot in range(start, start + width, STEP):
+                cols = slice(c * N + slot, c * N + slot + STEP)
                 nc.scalar.activation(lg[:, cols], e_rows[c][:, slot : slot + STEP], ACT.Ln, bias=one[:])
                 nc.vector.tensor_tensor(res[:, cols], lg[:, cols], v_rows[c][:, slot : slot + STEP], ALU.max)
-            nc.sync.dma_start(out_rows[:, first : first + width], res[:, first : first + width])
+            nc.sync.dma_start(out[0, c * P : (c + 1) * P, start : start + width], res[:, first : first + width])
             first += width

@@ -78,7 +78,7 @@ def tile_attend_bpr_topk_kernel(tc, qT, k_words, k_scales, ib, ps, offs, out):
         nc.vector.tensor_copy(picked_scales[:], scale_pool[:].bitcast(U8).indirect(offsets[:]))
         picked_rows = picked_scales[:].bitcast(I32)
         for r in range(4):
-            nc.sync.dma_start(key_scales[r:P:32, :], picked_rows[SCALE_ROW0 + r : SCALE_ROW0 + SCALE_ROWS : 4, :])
+            nc.scalar.dma_start(key_scales[r:P:32, :], picked_rows[SCALE_ROW0 + r : SCALE_ROW0 + SCALE_ROWS : 4, :])
         bias_row = reused.tile([P, N], F32, name="bias_row", align_bytes=64, offset=4 * T)
         nc.vector.tensor_copy(bias_row[:], bias_pool[:].indirect(offsets[:]))
 

@@ -23,8 +23,8 @@ SB = N // P
 BIAS_ROW = P - 1
 HALF = N // 2
 SCALE_ROWS = 16
-SCALE_ROW0 = 48
-ZERO_SPLIT = 256
+SCALE_ROW0 = P - SCALE_ROWS
+ZERO_SPLIT = 512
 STEP = 128
 STORES = (128, 128, 256, 256, 256)
 EXP_CAP = 2.0**60
@@ -38,15 +38,15 @@ def tile_attend_bpr_topk_kernel(tc, qT, k_words, k_scales, ib, ps, offs, out):
         psum = ctx.enter_context(tc.psum_pool(name="psum", bufs=1))
 
         offsets = sb.tile([P, N // 16], U16, name="offsets")
-        bias_pool = reused.tile([P, T], F32, name="bias_pool", align_bytes=64, offset=0)
+        bias_pool = sb.tile([P, T], F32, name="bias_pool", align_bytes=64)
         scale_pool = sb.tile([P, T // 4], I32, name="scale_pool", align_bytes=64)
         word_pool = sb.tile([P, T], I32, name="word_pool")
         q_raw = [sb.tile([P, PACK, P], F32, name=f"q_raw{c}", align_bytes=64) for c in range(QB)]
         pos_pairs = sb.tile([P, 2], F32, name="pos_pairs")
+        zero = sb.tile([P, 1], F32, name="zero")
         one = sb.tile([P, 1], F32, name="one")
         ident = sb.tile([P, P], F32, name="ident")
         key_scales = sb.tile([P, N // 4], I32, name="key_scales", align_bytes=64)
-        v = sb.tile([P, QB * N], F32, name="v")
         e = sb.tile([P, QB * N], F32, name="e")
         capped = sb.tile([P, QB * N], F32, name="capped")
         lg = sb.tile([P, QB * N], F32, name="lg")
@@ -56,77 +56,84 @@ def tile_attend_bpr_topk_kernel(tc, qT, k_words, k_scales, ib, ps, offs, out):
             nc.sync.dma_start(q_raw[c][:], qT[0, :, c * P : (c + 1) * P].rearrange("(p j) n -> p j n", j=PACK))
 
         nc.sync.dma_start(offsets[:], offs)
-        nc.scalar.dma_start(scale_pool[SCALE_ROW0 : SCALE_ROW0 + SCALE_ROWS, :], k_scales[0].bitcast(I32))
+        nc.scalar.dma_start(scale_pool[SCALE_ROW0:P, :], k_scales[0].bitcast(I32))
         load_queries(0)
         nc.scalar.dma_start(bias_pool[BIAS_ROW:P, :], ib[0:1, :])
         nc.sync.dma_start(pos_pairs[:], ps[0].rearrange("(p i) o -> p (i o)", i=2))
         nc.sync.dma_start(word_pool[:], k_words[0].rearrange("p n t -> p (n t)").bitcast(I32))
         load_queries(1)
 
-        for rows in (slice(0, SCALE_ROW0), slice(SCALE_ROW0 + SCALE_ROWS, P)):
-            nc.vector.memset(scale_pool[rows, 0 : T // 8 - 1], 0)
-            nc.vector.memset(scale_pool[rows, T // 8 - 1 : T // 4], 0)
+        nc.vector.memset(scale_pool[0:SCALE_ROW0, 0 : T // 8 - 1], 0)
+        nc.vector.memset(scale_pool[0:SCALE_ROW0, T // 8 - 1 : T // 4], 0)
         odd = ZERO_SPLIT // 2 - 1
         nc.vector.memset(bias_pool[0:BIAS_ROW, 0:odd], 0.0)
         nc.vector.memset(bias_pool[0:BIAS_ROW, odd:ZERO_SPLIT], 0.0)
-        nc.gpsimd.memset(one[:], 1.0)
+        nc.gpsimd.memset(zero[:], 0.0)
         make_identity(nc, ident[:])
         nc.gpsimd.memset(bias_pool[0:BIAS_ROW, ZERO_SPLIT:T], 0.0)
         nc.gpsimd.memset(key_scales[:], 0)
+        nc.scalar.activation(one[:], zero[:], ACT.Copy, bias=1.0)
 
         picked_scales = sb.tile([P, N], U8, name="picked_scales", align_bytes=64)
         nc.vector.tensor_copy(picked_scales[:], scale_pool[:].bitcast(U8).indirect(offsets[:]))
         picked_rows = picked_scales[:].bitcast(I32)
         for r in range(4):
-            nc.scalar.dma_start(key_scales[r:P:32, :], picked_rows[SCALE_ROW0 + r : SCALE_ROW0 + SCALE_ROWS : 4, :])
-        bias_row = reused.tile([P, N], F32, name="bias_row", align_bytes=64, offset=4 * T)
-        nc.vector.tensor_copy(bias_row[:], bias_pool[:].indirect(offsets[:]))
+            nc.sync.dma_start(key_scales[r:P:32, :], picked_rows[SCALE_ROW0 + r : P : 4, :])
+
+        bias_row = [
+            sb.tile([P, HALF], F32, name="bias_row0", align_bytes=64),
+            reused.tile([P, HALF], F32, name="bias_row1", align_bytes=64, offset=0),
+        ]
+        for h in range(2):
+            nc.scalar.activation(
+                bias_row[h][:], bias_pool[:].indirect(offsets[:, h * HALF // 16 : (h + 1) * HALF // 16]), ACT.Copy
+            )
 
         grouped = [
             sb.tile([P, P, PACK], BF16, name="grouped0", align_bytes=64),
-            reused.tile([P, P, PACK], BF16, name="grouped1", align_bytes=64, offset=4 * T),
+            reused.tile([P, P, PACK], BF16, name="grouped1", align_bytes=64, offset=0),
         ]
-        q_codes = reused.tile([P, NQ], U32, name="q_codes", align_bytes=64, offset=0)
+        q_codes = sb.tile([P, NQ], U32, name="q_codes", align_bytes=64)
         q_scales = sb.tile([P, NQ], U8, name="q_scales", align_bytes=64)
-        keys = reused.tile([P, N], U32, name="keys", align_bytes=64, offset=4 * NQ)
+        keys = sb.tile([P, N], U32, name="keys", align_bytes=64)
 
-        def quantise(c):
-            nc.scalar.activation(
+        def woven(c):
+            return (
                 grouped[c][:].rearrange("p (g i) j -> p g j i", i=4),
                 q_raw[c][:].rearrange("p j (g i) -> p g j i", i=4),
-                ACT.Copy,
             )
+
+        def quantise(c):
             nc.vector.quantize_mx(
                 out=q_codes[:, c * P : (c + 1) * P].bitcast(FP8X4),
                 scales=q_scales[:, c * P : (c + 1) * P],
                 in_=grouped[c][:].rearrange("p m j -> p (m j)"),
             )
 
+        nc.vector.tensor_copy(*woven(0))
         quantise(0)
 
         pos_spread = psum.tile([P, 2, P], F32, name="bank4")
         for i in range(2):
             nc.tensor.transpose(pos_spread[:, i], pos_pairs[:, i : i + 1].to_broadcast([P, P]), ident[:])
         pos_row = sb.tile([P, NQ], F32, name="pos_row")
-        for c in range(QB):
-            nc.scalar.copy(
-                pos_row[:, c * P : (c + 1) * P].rearrange("p (n i) -> p n i", i=2),
-                pos_spread[:, :, c * P // 2 : (c + 1) * P // 2].rearrange("p i n -> p n i"),
-            )
+        nc.scalar.copy(pos_row[:].rearrange("p (n i) -> p n i", i=2), pos_spread[:].rearrange("p i n -> p n i"))
 
         bias_cols = []
-        for b in range(SB):
-            turned = psum.tile([P, P], F32, name=f"bank{b}")
-            nc.tensor.transpose(turned[:], bias_row[:, b * P : (b + 1) * P], ident[:])
-            bias_col = sb.tile([P, 1], F32, name=f"bias_col{b}")
-            nc.scalar.copy(bias_col[:], turned[:, BIAS_ROW:P])
-            bias_cols.append(bias_col)
+        for h in range(2):
+            turned = psum.tile([P, 2, P], F32, name=f"bank{2 * h}")
+            for b in range(2):
+                nc.tensor.transpose(turned[:, b], bias_row[h][:, b * P : (b + 1) * P], ident[:])
+            pair = sb.tile([P, 2], F32, name=f"bias_pair{h}")
+            nc.scalar.copy(pair[:], turned[:, :, BIAS_ROW])
+            bias_cols.extend(pair[:, b : b + 1] for b in range(2))
 
         for h in range(2):
             nc.vector.tensor_copy(
                 keys[:, h * HALF : (h + 1) * HALF],
                 word_pool[:].bitcast(U32).indirect(offsets[:, h * HALF // 16 : (h + 1) * HALF // 16]),
             )
+        nc.scalar.activation(*woven(1), ACT.Copy)
         quantise(1)
 
         scores = []
@@ -145,9 +152,10 @@ def tile_attend_bpr_topk_kernel(tc, qT, k_words, k_scales, ib, ps, offs, out):
                 )
                 scores.append((acc, b, queries, slice(c * N + b * P, c * N + (b + 1) * P)))
 
+        v = sb.tile([P, QB * N], F32, name="v")
         for acc, b, queries, cols in scores:
             nc.vector.scalar_tensor_tensor(
-                v[:, cols], acc[:], bias_cols[b][:], pos_row[:, queries], ALU.add, ALU.subtract
+                v[:, cols], acc[:], bias_cols[b], pos_row[:, queries], ALU.add, ALU.subtract
             )
         for acc, b, queries, cols in scores:
             nc.scalar.activation(e[:, cols], v[:, cols], ACT.Exp)

@@ -38,7 +38,7 @@ def tile_attend_bpr_topk_kernel(tc, qT, k_words, k_scales, ib, ps, offs, out):
         psum = ctx.enter_context(tc.psum_pool(name="psum", bufs=1))
 
         offsets = sb.tile([P, N // 16], U16, name="offsets")
-        bias_pool = sb.tile([P, T], F32, name="bias_pool", align_bytes=64)
+        bias_pool = reused.tile([P, T], F32, name="bias_pool", align_bytes=64, offset=4 * HALF)
         scale_pool = sb.tile([P, T // 4], I32, name="scale_pool", align_bytes=64)
         word_pool = sb.tile([P, T], I32, name="word_pool")
         q_raw = [sb.tile([P, PACK, P], F32, name=f"q_raw{c}", align_bytes=64) for c in range(QB)]
@@ -84,16 +84,14 @@ def tile_attend_bpr_topk_kernel(tc, qT, k_words, k_scales, ib, ps, offs, out):
             sb.tile([P, HALF], F32, name="bias_row0", align_bytes=64),
             reused.tile([P, HALF], F32, name="bias_row1", align_bytes=64, offset=0),
         ]
-        for h in range(2):
-            nc.scalar.activation(
-                bias_row[h][:], bias_pool[:].indirect(offsets[:, h * HALF // 16 : (h + 1) * HALF // 16]), ACT.Copy
-            )
+        nc.scalar.activation(bias_row[0][:], bias_pool[:].indirect(offsets[:, 0 : HALF // 16]), ACT.Copy)
+        nc.vector.tensor_copy(bias_row[1][:], bias_pool[:].indirect(offsets[:, HALF // 16 : N // 16]))
 
         grouped = [
             sb.tile([P, P, PACK], BF16, name="grouped0", align_bytes=64),
             reused.tile([P, P, PACK], BF16, name="grouped1", align_bytes=64, offset=0),
         ]
-        q_codes = sb.tile([P, NQ], U32, name="q_codes", align_bytes=64)
+        q_codes = reused.tile([P, NQ], U32, name="q_codes", align_bytes=64, offset=4 * HALF)
         q_scales = sb.tile([P, NQ], U8, name="q_scales", align_bytes=64)
         keys = sb.tile([P, N], U32, name="keys", align_bytes=64)
 

@@ -23,8 +23,8 @@ SB = N // P
 BIAS_ROW = P - 1
 HALF = N // 2
 SCALE_ROWS = 16
-SCALE_ROW0 = P - SCALE_ROWS
-ZERO_SPLIT = 512
+SCALE_ROW0 = 48
+ZERO_SPLIT = 256
 STEP = 128
 STORES = (128, 128, 256, 256, 256)
 EXP_CAP = 2.0**60
@@ -56,15 +56,16 @@ def tile_attend_bpr_topk_kernel(tc, qT, k_words, k_scales, ib, ps, offs, out):
             nc.sync.dma_start(q_raw[c][:], qT[0, :, c * P : (c + 1) * P].rearrange("(p j) n -> p j n", j=PACK))
 
         nc.sync.dma_start(offsets[:], offs)
-        nc.scalar.dma_start(scale_pool[SCALE_ROW0:P, :], k_scales[0].bitcast(I32))
+        nc.scalar.dma_start(scale_pool[SCALE_ROW0 : SCALE_ROW0 + SCALE_ROWS, :], k_scales[0].bitcast(I32))
         load_queries(0)
         nc.scalar.dma_start(bias_pool[BIAS_ROW:P, :], ib[0:1, :])
         nc.sync.dma_start(pos_pairs[:], ps[0].rearrange("(p i) o -> p (i o)", i=2))
         nc.sync.dma_start(word_pool[:], k_words[0].rearrange("p n t -> p (n t)").bitcast(I32))
         load_queries(1)
 
-        nc.vector.memset(scale_pool[0:SCALE_ROW0, 0 : T // 8 - 1], 0)
-        nc.vector.memset(scale_pool[0:SCALE_ROW0, T // 8 - 1 : T // 4], 0)
+        for rows in (slice(0, SCALE_ROW0), slice(SCALE_ROW0 + SCALE_ROWS, P)):
+            nc.vector.memset(scale_pool[rows, 0 : T // 8 - 1], 0)
+            nc.vector.memset(scale_pool[rows, T // 8 - 1 : T // 4], 0)
         odd = ZERO_SPLIT // 2 - 1
         nc.vector.memset(bias_pool[0:BIAS_ROW, 0:odd], 0.0)
         nc.vector.memset(bias_pool[0:BIAS_ROW, odd:ZERO_SPLIT], 0.0)
@@ -78,7 +79,7 @@ def tile_attend_bpr_topk_kernel(tc, qT, k_words, k_scales, ib, ps, offs, out):
         nc.vector.tensor_copy(picked_scales[:], scale_pool[:].bitcast(U8).indirect(offsets[:]))
         picked_rows = picked_scales[:].bitcast(I32)
         for r in range(4):
-            nc.sync.dma_start(key_scales[r:P:32, :], picked_rows[SCALE_ROW0 + r : P : 4, :])
+            nc.sync.dma_start(key_scales[r:P:32, :], picked_rows[SCALE_ROW0 + r : SCALE_ROW0 + SCALE_ROWS : 4, :])
 
         bias_row = [
             sb.tile([P, HALF], F32, name="bias_row0", align_bytes=64),

@@ -38,11 +38,11 @@ def tile_attend_bpr_topk_kernel(tc, qT, k_words, k_scales, ib, ps, offs, out):
         psum = ctx.enter_context(tc.psum_pool(name="psum", bufs=1))
 
         offsets = sb.tile([P, N // 16], U16, name="offsets")
-        bias_pool = reused.tile([P, T], F32, name="bias_pool", align_bytes=64, offset=4 * HALF)
+        bias_pool = reused.tile([P, T], F32, name="bias_pool", align_bytes=64, offset=4 * HALF + 64)
         scale_pool = sb.tile([P, T // 4], I32, name="scale_pool", align_bytes=64)
         word_pool = sb.tile([P, T], I32, name="word_pool")
         q_raw = [sb.tile([P, PACK, P], F32, name=f"q_raw{c}", align_bytes=64) for c in range(QB)]
-        pos_pairs = sb.tile([P, 2], F32, name="pos_pairs")
+        pos_rows = sb.tile([P, P], F32, name="pos_rows")
         zero = sb.tile([P, 1], F32, name="zero")
         one = sb.tile([P, 1], F32, name="one")
         ident = sb.tile([P, P], F32, name="ident")
@@ -59,7 +59,7 @@ def tile_attend_bpr_topk_kernel(tc, qT, k_words, k_scales, ib, ps, offs, out):
         nc.scalar.dma_start(scale_pool[SCALE_ROW0 : SCALE_ROW0 + SCALE_ROWS, :], k_scales[0].bitcast(I32))
         load_queries(0)
         nc.scalar.dma_start(bias_pool[BIAS_ROW:P, :], ib[0:1, :])
-        nc.sync.dma_start(pos_pairs[:], ps[0].rearrange("(p i) o -> p (i o)", i=2))
+        nc.sync.dma_start(pos_rows[P - QB : P, :], ps[0].rearrange("(c n) o -> c (n o)", c=QB))
         nc.sync.dma_start(word_pool[:], k_words[0].rearrange("p n t -> p (n t)").bitcast(I32))
         load_queries(1)
 
@@ -69,6 +69,8 @@ def tile_attend_bpr_topk_kernel(tc, qT, k_words, k_scales, ib, ps, offs, out):
         odd = ZERO_SPLIT // 2 - 1
         nc.vector.memset(bias_pool[0:BIAS_ROW, 0:odd], 0.0)
         nc.vector.memset(bias_pool[0:BIAS_ROW, odd:ZERO_SPLIT], 0.0)
+        nc.vector.memset(pos_rows[0 : P - QB, 0 : P // 2 - 1], 0.0)
+        nc.vector.memset(pos_rows[0 : P - QB, P // 2 - 1 : P], 0.0)
         nc.gpsimd.memset(zero[:], 0.0)
         make_identity(nc, ident[:])
         nc.gpsimd.memset(bias_pool[0:BIAS_ROW, ZERO_SPLIT:T], 0.0)
@@ -83,16 +85,13 @@ def tile_attend_bpr_topk_kernel(tc, qT, k_words, k_scales, ib, ps, offs, out):
 
         bias_row = [
             sb.tile([P, HALF], F32, name="bias_row0", align_bytes=64),
-            reused.tile([P, HALF], F32, name="bias_row1", align_bytes=64, offset=0),
+            reused.tile([P, HALF], F32, name="bias_row1", align_bytes=64, offset=64),
         ]
         nc.scalar.activation(bias_row[0][:], bias_pool[:].indirect(offsets[:, 0 : HALF // 16]), ACT.Copy)
         nc.vector.tensor_copy(bias_row[1][:], bias_pool[:].indirect(offsets[:, HALF // 16 : N // 16]))
 
-        grouped = [
-            sb.tile([P, P, PACK], BF16, name="grouped0", align_bytes=64),
-            reused.tile([P, P, PACK], BF16, name="grouped1", align_bytes=64, offset=0),
-        ]
-        q_codes = reused.tile([P, NQ], U32, name="q_codes", align_bytes=64, offset=4 * HALF)
+        grouped = [sb.tile([P, P, PACK], BF16, name="grouped0", align_bytes=64)]
+        q_codes = reused.tile([P, NQ], U32, name="q_codes", align_bytes=64, offset=4 * HALF + 64)
         q_scales = sb.tile([P, NQ], U8, name="q_scales", align_bytes=64)
         keys = sb.tile([P, N], U32, name="keys", align_bytes=64)
 
@@ -112,11 +111,17 @@ def tile_attend_bpr_topk_kernel(tc, qT, k_words, k_scales, ib, ps, offs, out):
         nc.vector.tensor_copy(*woven(0))
         quantise(0)
 
-        pos_spread = psum.tile([P, 2, P], F32, name="bank4")
-        for i in range(2):
-            nc.tensor.transpose(pos_spread[:, i], pos_pairs[:, i : i + 1].to_broadcast([P, P]), ident[:])
+        pos_turned = psum.tile([P, P], F32, name="bank5")
+        nc.tensor.transpose(pos_turned[:], pos_rows[:], ident[:])
+        pos_cols = reused.tile([P, QB], F32, name="pos_cols", align_bytes=64, offset=0)
+        nc.scalar.copy(pos_cols[:], pos_turned[:, P - QB : P])
+        pos_spread = psum.tile([P, NQ], F32, name="bank4")
+        for c in range(QB):
+            nc.tensor.transpose(
+                pos_spread[:, c * P : (c + 1) * P], pos_cols[:, c : c + 1].to_broadcast([P, P]), ident[:]
+            )
         pos_row = sb.tile([P, NQ], F32, name="pos_row")
-        nc.scalar.copy(pos_row[:].rearrange("p (n i) -> p n i", i=2), pos_spread[:].rearrange("p i n -> p n i"))
+        nc.scalar.copy(pos_row[:], pos_spread[:])
 
         bias_cols = []
         for h in range(2):
@@ -132,6 +137,7 @@ def tile_attend_bpr_topk_kernel(tc, qT, k_words, k_scales, ib, ps, offs, out):
                 keys[:, h * HALF : (h + 1) * HALF],
                 word_pool[:].bitcast(U32).indirect(offsets[:, h * HALF // 16 : (h + 1) * HALF // 16]),
             )
+        grouped.append(reused.tile([P, P, PACK], BF16, name="grouped1", align_bytes=64, offset=0))
         nc.scalar.activation(*woven(1), ACT.Copy)
         quantise(1)
 

from contextlib import ExitStack

import concourse.mybir as mybir
from concourse.masks import make_identity

T, D, NQ, N = 2048, 512, 256, 512
FLOPS = 2 * NQ * N * D

F32 = mybir.dt.float32
BF16 = mybir.dt.bfloat16
I32 = mybir.dt.int32
U32 = mybir.dt.uint32
U16 = mybir.dt.uint16
U8 = mybir.dt.uint8
FP8X4 = mybir.dt.float8_e4m3fn_x4
ACT = mybir.ActivationFunctionType
ALU = mybir.AluOpType

P = 128
PACK = 4
QB = NQ // P
SB = N // P
BIAS_ROW = P - 1
HALF = N // 2
SCALE_ROWS = 16
SCALE_ROW0 = 48
ZERO_SPLIT = 256
STEP = 128
STORES = (128, 128, 256, 256, 256)
EXP_CAP = 2.0**60


def tile_attend_bpr_topk_kernel(tc, qT, k_words, k_scales, ib, ps, offs, out):
    nc = tc.nc
    with ExitStack() as ctx:
        sb = ctx.enter_context(tc.tile_pool(name="sb", bufs=1))
        reused = ctx.enter_context(tc.tile_pool(name="reused", bufs=1))
        psum = ctx.enter_context(tc.psum_pool(name="psum", bufs=1))

        offsets = sb.tile([P, N // 16], U16, name="offsets")
        bias_pool = reused.tile([P, T], F32, name="bias_pool", align_bytes=64, offset=4 * HALF + 64)
        scale_pool = sb.tile([P, T // 4], I32, name="scale_pool", align_bytes=64)
        word_pool = sb.tile([P, T], I32, name="word_pool")
        q_raw = [sb.tile([P, PACK, P], F32, name=f"q_raw{c}", align_bytes=64) for c in range(QB)]
        pos_rows = sb.tile([P, P], F32, name="pos_rows")
        zero = sb.tile([P, 1], F32, name="zero")
        one = sb.tile([P, 1], F32, name="one")
        ident = sb.tile([P, P], F32, name="ident")
        key_scales = sb.tile([P, N // 4], I32, name="key_scales", align_bytes=64)
        e = sb.tile([P, QB * N], F32, name="e")
        capped = sb.tile([P, QB * N], F32, name="capped")
        lg = sb.tile([P, QB * N], F32, name="lg")
        res = sb.tile([P, QB * N], F32, name="res")

        def load_queries(c):
            nc.sync.dma_start(q_raw[c][:], qT[0, :, c * P : (c + 1) * P].rearrange("(p j) n -> p j n", j=PACK))

        nc.sync.dma_start(offsets[:], offs)
        nc.scalar.dma_start(scale_pool[SCALE_ROW0 : SCALE_ROW0 + SCALE_ROWS, :], k_scales[0].bitcast(I32))
        load_queries(0)
        nc.scalar.dma_start(bias_pool[BIAS_ROW:P, :], ib[0:1, :])
        nc.sync.dma_start(pos_rows[P - QB : P, :], ps[0].rearrange("(c n) o -> c (n o)", c=QB))
        nc.sync.dma_start(word_pool[:], k_words[0].rearrange("p n t -> p (n t)").bitcast(I32))
        load_queries(1)

        for rows in (slice(0, SCALE_ROW0), slice(SCALE_ROW0 + SCALE_ROWS, P)):
            nc.vector.memset(scale_pool[rows, 0 : T // 8 - 1], 0)
            nc.vector.memset(scale_pool[rows, T // 8 - 1 : T // 4], 0)
        odd = ZERO_SPLIT // 2 - 1
        nc.vector.memset(bias_pool[0:BIAS_ROW, 0:odd], 0.0)
        nc.vector.memset(bias_pool[0:BIAS_ROW, odd:ZERO_SPLIT], 0.0)
        nc.vector.memset(pos_rows[0 : P - QB, 0 : P // 2 - 1], 0.0)
        nc.vector.memset(pos_rows[0 : P - QB, P // 2 - 1 : P], 0.0)
        nc.gpsimd.memset(zero[:], 0.0)
        make_identity(nc, ident[:])
        nc.gpsimd.memset(bias_pool[0:BIAS_ROW, ZERO_SPLIT:T], 0.0)
        nc.gpsimd.memset(key_scales[:], 0)
        nc.scalar.activation(one[:], zero[:], ACT.Copy, bias=1.0)

        picked_scales = sb.tile([P, N], U8, name="picked_scales", align_bytes=64)
        nc.vector.tensor_copy(picked_scales[:], scale_pool[:].bitcast(U8).indirect(offsets[:]))
        picked_rows = picked_scales[:].bitcast(I32)
        for r in range(4):
            nc.sync.dma_start(key_scales[r:P:32, :], picked_rows[SCALE_ROW0 + r : SCALE_ROW0 + SCALE_ROWS : 4, :])

        bias_row = [
            sb.tile([P, HALF], F32, name="bias_row0", align_bytes=64),
            reused.tile([P, HALF], F32, name="bias_row1", align_bytes=64, offset=64),
        ]
        nc.scalar.activation(bias_row[0][:], bias_pool[:].indirect(offsets[:, 0 : HALF // 16]), ACT.Copy)
        nc.vector.tensor_copy(bias_row[1][:], bias_pool[:].indirect(offsets[:, HALF // 16 : N // 16]))

        grouped = [sb.tile([P, P, PACK], BF16, name="grouped0", align_bytes=64)]
        q_codes = reused.tile([P, NQ], U32, name="q_codes", align_bytes=64, offset=4 * HALF + 64)
        q_scales = sb.tile([P, NQ], U8, name="q_scales", align_bytes=64)
        keys = sb.tile([P, N], U32, name="keys", align_bytes=64)

        def woven(c):
            return (
                grouped[c][:].rearrange("p (g i) j -> p g j i", i=4),
                q_raw[c][:].rearrange("p j (g i) -> p g j i", i=4),
            )

        def quantise(c):
            nc.vector.quantize_mx(
                out=q_codes[:, c * P : (c + 1) * P].bitcast(FP8X4),
                scales=q_scales[:, c * P : (c + 1) * P],
                in_=grouped[c][:].rearrange("p m j -> p (m j)"),
            )

        nc.vector.tensor_copy(*woven(0))
        quantise(0)

        pos_turned = psum.tile([P, P], F32, name="bank5")
        nc.tensor.transpose(pos_turned[:], pos_rows[:], ident[:])
        pos_cols = reused.tile([P, QB], F32, name="pos_cols", align_bytes=64, offset=0)
        nc.scalar.copy(pos_cols[:], pos_turned[:, P - QB : P])
        pos_spread = psum.tile([P, NQ], F32, name="bank4")
        for c in range(QB):
            nc.tensor.transpose(
                pos_spread[:, c * P : (c + 1) * P], pos_cols[:, c : c + 1].to_broadcast([P, P]), ident[:]
            )
        pos_row = sb.tile([P, NQ], F32, name="pos_row")
        nc.scalar.copy(pos_row[:], pos_spread[:])

        bias_cols = []
        for h in range(2):
            turned = psum.tile([P, 2, P], F32, name=f"bank{2 * h}")
            for b in range(2):
                nc.tensor.transpose(turned[:, b], bias_row[h][:, b * P : (b + 1) * P], ident[:])
            pair = sb.tile([P, 2], F32, name=f"bias_pair{h}")
            nc.scalar.copy(pair[:], turned[:, :, BIAS_ROW])
            bias_cols.extend(pair[:, b : b + 1] for b in range(2))

        for h in range(2):
            nc.vector.tensor_copy(
                keys[:, h * HALF : (h + 1) * HALF],
                word_pool[:].bitcast(U32).indirect(offsets[:, h * HALF // 16 : (h + 1) * HALF // 16]),
            )
        grouped.append(reused.tile([P, P, PACK], BF16, name="grouped1", align_bytes=64, offset=0))
        nc.scalar.activation(*woven(1), ACT.Copy)
        quantise(1)

        scores = []
        for c in range(QB):
            queries = slice(c * P, (c + 1) * P)
            for b in range(SB):
                acc = psum.tile([P, P], F32, name=f"bank{c * SB + b}")
                nc.tensor.matmul_mx(
                    out=acc[:],
                    lhsT=keys[:, b * P : (b + 1) * P].bitcast(FP8X4),
                    lhsT_scale=key_scales[:].bitcast(U8)[:, b * P : (b + 1) * P],
                    rhs=q_codes[:, queries].bitcast(FP8X4),
                    rhs_scale=q_scales[:, queries],
                    start=True,
                    stop=True,
                )
                scores.append((acc, b, queries, slice(c * N + b * P, c * N + (b + 1) * P)))

        v = sb.tile([P, QB * N], F32, name="v")
        for acc, b, queries, cols in scores:
            nc.vector.scalar_tensor_tensor(
                v[:, cols], acc[:], bias_cols[b], pos_row[:, queries], ALU.add, ALU.subtract
            )
        for acc, b, queries, cols in scores:
            nc.scalar.activation(e[:, cols], v[:, cols], ACT.Exp)

        v_rows = []
        for c in range(QB):
            v_bank = psum.tile([P, N], F32, name=f"bank{c}")
            for b in range(SB):
                nc.tensor.transpose(v_bank[:, b * P : (b + 1) * P], v[:, c * N + b * P : c * N + (b + 1) * P], ident[:])
            v_rows.append(v_bank)
        e_rows = []
        for c in range(QB):
            nc.vector.tensor_scalar_min(capped[:, c * N : (c + 1) * N], e[:, c * N : (c + 1) * N], EXP_CAP)
            e_bank = psum.tile([P, N], F32, name=f"bank{QB + c}")
            for b in range(SB):
                nc.tensor.transpose(e_bank[:, b * P : (b + 1) * P], capped[:, c * N + b * P : c * N + (b + 1) * P], ident[:])
            e_rows.append(e_bank)

        first = 0
        for width in STORES:
            c, start = divmod(first, N)
            for slot in range(start, start + width, STEP):
                cols = slice(c * N + slot, c * N + slot + STEP)
                nc.scalar.activation(lg[:, cols], e_rows[c][:, slot : slot + STEP], ACT.Ln, bias=one[:])
                nc.vector.tensor_tensor(res[:, cols], lg[:, cols], v_rows[c][:, slot : slot + STEP], ALU.max)
            nc.sync.dma_start(out[0, c * P : (c + 1) * P, start : start + width], res[:, first : first + width])
            first += width
